import numpy as np
import ml_dtypes


def mxq(x, axis, fmt="e4m3"):
    dtype, down = {"e4m3": (ml_dtypes.float8_e4m3fn, 7), "e5m2": (ml_dtypes.float8_e5m2, 14)}[fmt]
    v = np.moveaxis(np.asarray(x, np.float32).astype(ml_dtypes.bfloat16).astype(np.float64), axis, -1)
    blocks = v.reshape(v.shape[:-1] + (-1, 32))
    amax = np.abs(blocks).max(-1, keepdims=True)
    byte = np.maximum(np.where(amax > 0, np.frexp(amax)[1] - 1 + 127, 0) - down, 1)
    scale = np.exp2(byte - 127.0)
    codes = (blocks / scale).astype(np.float32).astype(dtype).astype(np.float64)
    return np.moveaxis((codes * scale).reshape(v.shape), -1, axis)


WIDE = False


def mx_kscale(k):
    if not WIDE:
        return np.ones(k)
    levels = np.array([10, -10, 5, -5, 0])
    if k % 512:
        return np.exp2(np.random.permutation(np.resize(levels, k // 32))).repeat(32)
    a = np.empty((k // 512, 16))
    for p in range(k // 512):
        a[p, :8] = np.random.permutation(np.resize(levels, 8))
        for g in range(8):
            far = levels[np.abs(levels - a[p, g]) >= 10]
            a[p, g + 8] = far[np.random.randint(len(far))]
    return np.exp2(a.ravel()).repeat(32)


def f64(x):
    return np.asarray(x).astype(np.float64)


def striped(idx):
    return np.tile(idx.reshape(-1, 16).T, (8, 1)).astype(np.uint16)


def unstriped(offs):
    return offs[:16].T.reshape(-1).astype(np.int64)


def pack_weight(w):
    k, n = w.shape
    w = f64(np.asarray(w, np.float32).astype(ml_dtypes.bfloat16)).reshape(k // 32, 32, n)
    amax = np.abs(w).max(1)
    byte = np.clip(np.where(amax > 0, np.frexp(amax)[1] - 1 + 127 - 7, 1), 1, 254)
    scaled = (w * np.exp2(127.0 - byte)[:, None, :]).reshape(k, n).astype(np.float32)
    words = np.ascontiguousarray(scaled.reshape(k // 512, 128, 4, n).transpose(0, 1, 3, 2)).astype(ml_dtypes.float8_e4m3fn).view(np.uint8)
    return words, np.ascontiguousarray(byte.astype(np.uint8).reshape(k // 512, 16, n))


def unpack_weight(words, scales):
    g, p, n, _ = words.shape
    vals = np.ascontiguousarray(words).view(ml_dtypes.float8_e4m3fn).astype(np.float64) * np.repeat(np.exp2(scales.astype(np.float64) - 127.0), 8, axis=1)[..., None]
    return vals.transpose(0, 1, 3, 2).reshape(g * 512, n)


K, T, D, S, V, N = 2048, 512, 4, 1024, 256, 128


def setup_inputs():
    n = np.random.standard_normal
    s = mx_kscale(K)[:, None]
    words, scales = pack_weight(n((K, N)) / np.sqrt(K) / s)
    return {
        "xT": (n((K, T)) * s).astype(np.float32),
        "w_words": words,
        "w_scales": scales,
        "gate": np.tile(np.random.uniform(0.2, 1.0, (D, 1, V)) / np.sqrt(D), (1, N, 1)).astype(np.float32),
        "pos1": striped(np.random.permutation(T)[:V]),
        "pos2": striped(np.random.permutation(T)[:V]),
        "pos3": striped(np.random.permutation(T)[:V]),
        "pos4": striped(np.random.permutation(T)[:V]),
    }


def reference(xT, w_words, w_scales, gate, pos1, pos2, pos3, pos4):
    w = unpack_weight(w_words, w_scales)
    y = w.T @ mxq(f64(xT), 0, "e4m3")
    return sum(f64(gate[d]) * y[:, unstriped(p)] for d, p in enumerate((pos1, pos2, pos3, pos4)))

@@ -1,0 +1,123 @@
+from contextlib import ExitStack
+
+import concourse.mybir as mybir
+
+K, T, D, V, M = 2048, 512, 4, 256, 128
+FLOPS = 2 * K * M * T + 2 * D * M * V
+
+F32 = mybir.dt.float32
+BF16 = mybir.dt.bfloat16
+I32 = mybir.dt.int32
+U32 = mybir.dt.uint32
+U16 = mybir.dt.uint16
+U8 = mybir.dt.uint8
+FP8X4 = mybir.dt.float8_e4m3fn_x4
+MULT = mybir.AluOpType.mult
+ADD = mybir.AluOpType.add
+
+P = 128
+PACK = 4
+K_PASS = P * PACK
+PASSES = K // K_PASS
+GROUPS = ((0, 256), (256, 384), (384, 512))
+WIDE = ((0, 512, ((0, 256), (256, 320)), ((320, 512),), ((0, 256), (256, 512))),)
+LAST = (
+    (0, 256, ((0, 160),), ((160, 256),), ((0, 256),)),
+    (256, 384, ((256, 336),), ((336, 384),), ((256, 384),)),
+    (384, 512, ((384, 464),), ((464, 512),), ((384, 512),)),
+)
+
+
+def tile_picked_agg_lin_none_sub_l_kernel(tc, xT, w_words, w_scales, gate, pos1, pos2, pos3, pos4, out):
+    nc = tc.nc
+    with ExitStack() as ctx:
+        keep = ctx.enter_context(tc.tile_pool(name="keep", bufs=1))
+        psum = ctx.enter_context(tc.psum_pool(name="psum", bufs=1))
+
+        lists = [keep.tile([P, V // 16], U16, name=f"list{d}") for d in range(D)]
+        w_codes = keep.tile([P, PASSES, M], U32, align_bytes=64)
+        w_plane = keep.tile([P, PASSES, M], U8, align_bytes=64)
+        gates = keep.tile([P, D, V], F32)
+        y = keep.tile([P, T], F32)
+        banks = [psum.tile([P, hi - lo], F32, name=f"bank{lo}") for lo, hi in GROUPS]
+
+        nc.gpsimd.memset(w_plane[:].bitcast(I32), 0)
+        for q in range(4):
+            nc.gpsimd.dma_start(
+                out=w_plane[32 * q : 32 * q + 4, :, :].bitcast(I32),
+                in_=w_scales[:, 4 * q : 4 * q + 4, :].rearrange("a r m -> r a m").bitcast(I32),
+            )
+
+        raws = {}
+        for a in range(PASSES):
+            rows = xT[a * K_PASS : (a + 1) * K_PASS, :].rearrange("(p j) t -> p j t", j=PACK)
+            for lo, hi, vec, sca, quant in (LAST if a == PASSES - 1 else WIDE):
+                raw = keep.tile([P, PACK, hi - lo], F32, name=f"raw{a}_{lo}")
+                nc.sync.dma_start(out=raw[:], in_=rows[:, :, lo:hi])
+                raws[(a, lo)] = raw
+            if a == 0:
+                nc.sync.dma_start(out=w_codes[:].bitcast(I32), in_=w_words.rearrange("a p m r -> p a (m r)").bitcast(I32))
+        gate_rows = gate.rearrange("d m v -> m d v")
+        nc.sync.dma_start(lists[0][:], pos1)
+        nc.sync.dma_start(lists[1][:], pos2)
+        nc.sync.dma_start(out=gates[:, 0:2, :], in_=gate_rows[:, 0:2, :])
+        nc.sync.dma_start(lists[2][:], pos3)
+        nc.sync.dma_start(lists[3][:], pos4)
+        nc.sync.dma_start(out=gates[:, 2:4, :], in_=gate_rows[:, 2:4, :])
+
+        for a in range(PASSES):
+            grouped = keep.tile([P, T, PACK], BF16, align_bytes=64, name=f"grouped{a}")
+            codes = keep.tile([P, T], U32, align_bytes=64, name=f"codes{a}")
+            plane = keep.tile([P, T], U8, align_bytes=64, name=f"plane{a}")
+            for lo, hi, vec, sca, quant in (LAST if a == PASSES - 1 else WIDE):
+                raw = raws[(a, lo)]
+                for c0, c1 in sca:
+                    nc.scalar.copy(
+                        out=grouped[:, c0:c1, :].rearrange("p (c i) j -> p c j i", i=4),
+                        in_=raw[:, :, c0 - lo : c1 - lo].rearrange("p j (c i) -> p c j i", i=4),
+                    )
+                for c0, c1 in vec:
+                    nc.vector.tensor_copy(
+                        out=grouped[:, c0:c1, :].rearrange("p (c i) j -> p c j i", i=4),
+                        in_=raw[:, :, c0 - lo : c1 - lo].rearrange("p j (c i) -> p c j i", i=4),
+                    )
+                for c0, c1 in quant:
+                    nc.vector.quantize_mx(
+                        out=codes[:, c0:c1].bitcast(FP8X4),
+                        scales=plane[:, c0:c1],
+                        in_=grouped[:, c0:c1, :].rearrange("p c j -> p (c j)"),
+                    )
+                for bank, (g0, g1) in zip(banks, GROUPS):
+                    if lo <= g0 and g1 <= hi:
+                        nc.tensor.matmul_mx(
+                            out=bank[:],
+                            lhsT=w_codes[:, a, :].bitcast(FP8X4),
+                            lhsT_scale=w_plane[:, a, :],
+                            rhs=codes[:, g0:g1].bitcast(FP8X4),
+                            rhs_scale=plane[:, g0:g1],
+                            start=(a == 0),
+                            stop=(a == PASSES - 1),
+                        )
+                        if a == PASSES - 1:
+                            nc.scalar.copy(out=y[:, g0:g1], in_=bank[:])
+
+        picked = [keep.tile([P, V], F32, name=f"picked{d}") for d in range(D)]
+        sum2 = keep.tile([P, V], F32)
+        sum3 = keep.tile([P, V], F32)
+        result = keep.tile([P, V], F32)
+        H = V // 2
+
+        def gather(d, v0, v1):
+            nc.vector.tensor_tensor(picked[d][:, v0:v1], y[:].indirect(lists[d][:, v0 // 16 : v1 // 16]), gates[:, d, v0:v1], MULT)
+
+        gather(0, 0, V)
+        gather(1, 0, V)
+        gather(2, 0, V)
+        nc.vector.tensor_tensor(sum2[:], picked[0][:], picked[1][:], ADD)
+        gather(3, 0, H)
+        nc.vector.tensor_tensor(sum3[:], sum2[:], picked[2][:], ADD)
+        gather(3, H, V)
+        nc.vector.tensor_tensor(result[:, 0:H], sum3[:, 0:H], picked[3][:, 0:H], ADD)
+        nc.sync.dma_start(out=out[:, 0:H], in_=result[:, 0:H])
+        nc.vector.tensor_tensor(result[:, H:V], sum3[:, H:V], picked[3][:, H:V], ADD)
+        nc.scalar.dma_start(out=out[:, H:V], in_=result[:, H:V])

@@ -22,9 +22,9 @@ PASSES = K // K_PASS
 GROUPS = ((0, 256), (256, 384), (384, 512))
 WIDE = ((0, 512, ((0, 256), (256, 320)), ((320, 512),), ((0, 256), (256, 512))),)
 LAST = (
-    (0, 256, ((0, 160),), ((160, 256),), ((0, 256),)),
-    (256, 384, ((256, 336),), ((336, 384),), ((256, 384),)),
-    (384, 512, ((384, 464),), ((464, 512),), ((384, 512),)),
+    (0, 256, ((0, 168),), ((168, 256),), ((0, 256),)),
+    (256, 384, ((256, 340),), ((340, 384),), ((256, 384),)),
+    (384, 512, ((384, 468),), ((468, 512),), ((384, 512),)),
 )
 
 
@@ -48,6 +48,8 @@ def tile_picked_agg_lin_none_sub_l_kernel(tc, xT, w_words, w_scales, gate, pos1,
                 in_=w_scales[:, 4 * q : 4 * q + 4, :].rearrange("a r m -> r a m").bitcast(I32),
             )
 
+        w_rows = w_words.rearrange("a p m r -> p a (m r)").bitcast(I32)
+        nc.scalar.dma_start(out=w_codes[:, 0:3, :].bitcast(I32), in_=w_rows[:, 0:3, :])
         raws = {}
         for a in range(PASSES):
             rows = xT[a * K_PASS : (a + 1) * K_PASS, :].rearrange("(p j) t -> p j t", j=PACK)
@@ -55,8 +57,7 @@ def tile_picked_agg_lin_none_sub_l_kernel(tc, xT, w_words, w_scales, gate, pos1,
                 raw = keep.tile([P, PACK, hi - lo], F32, name=f"raw{a}_{lo}")
                 nc.sync.dma_start(out=raw[:], in_=rows[:, :, lo:hi])
                 raws[(a, lo)] = raw
-            if a == 0:
-                nc.sync.dma_start(out=w_codes[:].bitcast(I32), in_=w_words.rearrange("a p m r -> p a (m r)").bitcast(I32))
+        nc.sync.dma_start(out=w_codes[:, 3, :].bitcast(I32), in_=w_rows[:, 3, :])
         gate_rows = gate.rearrange("d m v -> m d v")
         nc.sync.dma_start(lists[0][:], pos1)
         nc.sync.dma_start(lists[1][:], pos2)
@@ -73,13 +74,13 @@ def tile_picked_agg_lin_none_sub_l_kernel(tc, xT, w_words, w_scales, gate, pos1,
                 raw = raws[(a, lo)]
                 for c0, c1 in sca:
                     nc.scalar.copy(
-                        out=grouped[:, c0:c1, :].rearrange("p (c i) j -> p c j i", i=4),
-                        in_=raw[:, :, c0 - lo : c1 - lo].rearrange("p j (c i) -> p c j i", i=4),
+                        out=grouped[:, c0:c1, :],
+                        in_=raw[:, :, c0 - lo : c1 - lo].rearrange("p j c -> p c j"),
                     )
                 for c0, c1 in vec:
                     nc.vector.tensor_copy(
-                        out=grouped[:, c0:c1, :].rearrange("p (c i) j -> p c j i", i=4),
-                        in_=raw[:, :, c0 - lo : c1 - lo].rearrange("p j (c i) -> p c j i", i=4),
+                        out=grouped[:, c0:c1, :],
+                        in_=raw[:, :, c0 - lo : c1 - lo].rearrange("p j c -> p c j"),
                     )
                 for c0, c1 in quant:
                     nc.vector.quantize_mx(
@@ -118,6 +119,6 @@ def tile_picked_agg_lin_none_sub_l_kernel(tc, xT, w_words, w_scales, gate, pos1,
         nc.vector.tensor_tensor(sum3[:], sum2[:], picked[2][:], ADD)
         gather(3, H, V)
         nc.vector.tensor_tensor(result[:, 0:H], sum3[:, 0:H], picked[3][:, 0:H], ADD)
-        nc.sync.dma_start(out=out[:, 0:H], in_=result[:, 0:H])
+        nc.scalar.dma_start(out=out[:, 0:H], in_=result[:, 0:H])
         nc.vector.tensor_tensor(result[:, H:V], sum3[:, H:V], picked[3][:, H:V], ADD)
-        nc.scalar.dma_start(out=out[:, H:V], in_=result[:, H:V])
+        nc.sync.dma_start(out=out[:, H:V], in_=result[:, H:V])

@@ -1,6 +1,7 @@
 from contextlib import ExitStack
 
 import concourse.mybir as mybir
+from concourse.masks import make_identity
 
 K, T, D, V, M = 2048, 512, 4, 256, 128
 FLOPS = 2 * K * M * T + 2 * D * M * V
@@ -14,17 +15,21 @@ U8 = mybir.dt.uint8
 FP8X4 = mybir.dt.float8_e4m3fn_x4
 MULT = mybir.AluOpType.mult
 ADD = mybir.AluOpType.add
+COPY = mybir.ActivationFunctionType.Copy
 
 P = 128
 PACK = 4
 K_PASS = P * PACK
 PASSES = K // K_PASS
+H = V // 2
 GROUPS = ((0, 256), (256, 384), (384, 512))
-WIDE = ((0, 512, ((0, 256), (256, 320)), ((320, 512),), ((0, 256), (256, 512))),)
-LAST = (
-    (0, 256, ((0, 168),), ((168, 256),), ((0, 256),)),
-    (256, 384, ((256, 340),), ((340, 384),), ((256, 384),)),
-    (384, 512, ((384, 468),), ((468, 512),), ((384, 512),)),
+LOADS = (
+    (0, 0, 4, 0, 512, ((0, 256), (256, 320)), ((320, 512),), ((0, 256), (256, 512)), ((0, 0), (0, 1), (0, 2))),
+    (1, 0, 4, 0, 512, ((0, 256), (256, 320)), ((320, 512),), ((0, 256), (256, 512)), ((1, 0), (1, 1), (1, 2))),
+    (2, 0, 4, 0, 512, ((0, 256), (256, 320)), ((320, 512),), ((0, 256), (256, 512)), ((2, 0), (2, 1), (2, 2))),
+    (3, 0, 4, 0, 256, ((0, 168),), ((168, 256),), ((0, 256),), ((3, 0),)),
+    (3, 0, 4, 256, 384, ((256, 340),), ((340, 384),), ((256, 384),), ((3, 1),)),
+    (3, 0, 4, 384, 512, ((384, 468),), ((468, 512),), ((384, 512),), ((3, 2),)),
 )
 
 
@@ -37,88 +42,129 @@ def tile_picked_agg_lin_none_sub_l_kernel(tc, xT, w_words, w_scales, gate, pos1,
         lists = [keep.tile([P, V // 16], U16, name=f"list{d}") for d in range(D)]
         w_codes = keep.tile([P, PASSES, M], U32, align_bytes=64)
         w_plane = keep.tile([P, PASSES, M], U8, align_bytes=64)
-        gates = keep.tile([P, D, V], F32)
         y = keep.tile([P, T], F32)
-        banks = [psum.tile([P, hi - lo], F32, name=f"bank{lo}") for lo, hi in GROUPS]
-
-        nc.gpsimd.memset(w_plane[:].bitcast(I32), 0)
-        for q in range(4):
-            nc.gpsimd.dma_start(
-                out=w_plane[32 * q : 32 * q + 4, :, :].bitcast(I32),
-                in_=w_scales[:, 4 * q : 4 * q + 4, :].rearrange("a r m -> r a m").bitcast(I32),
-            )
-
+        banks = [psum.tile([P, 512], F32, name=f"bank{b}") for b in range(8)]
         w_rows = w_words.rearrange("a p m r -> p a (m r)").bitcast(I32)
-        nc.scalar.dma_start(out=w_codes[:, 0:3, :].bitcast(I32), in_=w_rows[:, 0:3, :])
-        raws = {}
-        for a in range(PASSES):
-            rows = xT[a * K_PASS : (a + 1) * K_PASS, :].rearrange("(p j) t -> p j t", j=PACK)
-            for lo, hi, vec, sca, quant in (LAST if a == PASSES - 1 else WIDE):
-                raw = keep.tile([P, PACK, hi - lo], F32, name=f"raw{a}_{lo}")
-                nc.sync.dma_start(out=raw[:], in_=rows[:, :, lo:hi])
-                raws[(a, lo)] = raw
-        nc.sync.dma_start(out=w_codes[:, 3, :].bitcast(I32), in_=w_rows[:, 3, :])
         gate_rows = gate.rearrange("d m v -> m d v")
+
+        def load_x(n):
+            a, j0, j1, lo, hi = LOADS[n][0:5]
+            rows = xT[a * K_PASS : (a + 1) * K_PASS, :].rearrange("(p j) t -> p j t", j=PACK)
+            raw = keep.tile([P, j1 - j0, hi - lo], F32, name=f"raw{n}")
+            nc.sync.dma_start(out=raw[:], in_=rows[:, j0:j1, lo:hi])
+            return raw
+
+        def load_scales(queue):
+            for q in range(4):
+                queue.dma_start(
+                    out=w_plane[32 * q : 32 * q + 4, :, :].bitcast(I32),
+                    in_=w_scales[:, 4 * q : 4 * q + 4, :].rearrange("a r m -> r a m").bitcast(I32),
+                )
+
+        gate_cols = keep.tile([P, 4], F32)
+        ident = keep.tile([P, P], F32)
+        gates = keep.tile([P, D, V], F32)
+        nc.gpsimd.memset(w_plane[:].bitcast(I32), 0)
+        load_scales(nc.gpsimd)
+        make_identity(nc, ident[:])
+        nc.scalar.dma_start(out=w_codes[:, 0:3, :].bitcast(I32), in_=w_rows[:, 0:3, :])
+        raws = [load_x(n) for n in range(len(LOADS))]
+        nc.sync.dma_start(out=w_codes[:, 3, :].bitcast(I32), in_=w_rows[:, 3, :])
         nc.sync.dma_start(lists[0][:], pos1)
         nc.sync.dma_start(lists[1][:], pos2)
-        nc.sync.dma_start(out=gates[:, 0:2, :], in_=gate_rows[:, 0:2, :])
+        with nc.allow_non_contiguous_dma(reason="one gate value a partition"):
+            nc.sync.dma_start(out=gate_cols[:], in_=gate.rearrange("d m (h p) -> (d m h) p", h=2)[0 : 4 * 129 : 129, :].rearrange("i p -> p i"))
         nc.sync.dma_start(lists[2][:], pos3)
-        nc.sync.dma_start(lists[3][:], pos4)
         nc.sync.dma_start(out=gates[:, 2:4, :], in_=gate_rows[:, 2:4, :])
+        nc.sync.dma_start(lists[3][:], pos4)
 
-        for a in range(PASSES):
-            grouped = keep.tile([P, T, PACK], BF16, align_bytes=64, name=f"grouped{a}")
-            codes = keep.tile([P, T], U32, align_bytes=64, name=f"codes{a}")
-            plane = keep.tile([P, T], U8, align_bytes=64, name=f"plane{a}")
-            for lo, hi, vec, sca, quant in (LAST if a == PASSES - 1 else WIDE):
-                raw = raws[(a, lo)]
-                for c0, c1 in sca:
-                    nc.scalar.copy(
-                        out=grouped[:, c0:c1, :],
-                        in_=raw[:, :, c0 - lo : c1 - lo].rearrange("p j c -> p c j"),
-                    )
-                for c0, c1 in vec:
-                    nc.vector.tensor_copy(
-                        out=grouped[:, c0:c1, :],
-                        in_=raw[:, :, c0 - lo : c1 - lo].rearrange("p j c -> p c j"),
-                    )
-                for c0, c1 in quant:
-                    nc.vector.quantize_mx(
-                        out=codes[:, c0:c1].bitcast(FP8X4),
-                        scales=plane[:, c0:c1],
-                        in_=grouped[:, c0:c1, :].rearrange("p c j -> p (c j)"),
-                    )
-                for bank, (g0, g1) in zip(banks, GROUPS):
-                    if lo <= g0 and g1 <= hi:
-                        nc.tensor.matmul_mx(
-                            out=bank[:],
-                            lhsT=w_codes[:, a, :].bitcast(FP8X4),
-                            lhsT_scale=w_plane[:, a, :],
-                            rhs=codes[:, g0:g1].bitcast(FP8X4),
-                            rhs_scale=plane[:, g0:g1],
-                            start=(a == 0),
-                            stop=(a == PASSES - 1),
-                        )
-                        if a == PASSES - 1:
-                            nc.scalar.copy(out=y[:, g0:g1], in_=bank[:])
+        grouped = [keep.tile([P, T, PACK], BF16, align_bytes=64, name=f"grouped{a}") for a in range(PASSES)]
+        codes = [keep.tile([P, T], U32, align_bytes=64, name=f"codes{a}") for a in range(PASSES)]
+        planes = [keep.tile([P, T], U8, align_bytes=64, name=f"plane{a}") for a in range(PASSES)]
+        for raw, (a, j0, j1, lo, hi, vec, sca, quant, mult) in zip(raws, LOADS):
+            for c0, c1 in sca:
+                nc.scalar.copy(
+                    out=grouped[a][:, c0:c1, j0:j1],
+                    in_=raw[:, :, c0 - lo : c1 - lo].rearrange("p j c -> p c j"),
+                )
+            for c0, c1 in vec:
+                nc.vector.tensor_copy(
+                    out=grouped[a][:, c0:c1, j0:j1],
+                    in_=raw[:, :, c0 - lo : c1 - lo].rearrange("p j c -> p c j"),
+                )
+            for c0, c1 in quant:
+                nc.vector.quantize_mx(
+                    out=codes[a][:, c0:c1].bitcast(FP8X4),
+                    scales=planes[a][:, c0:c1],
+                    in_=grouped[a][:, c0:c1, :].rearrange("p c j -> p (c j)"),
+                )
+            for b, g in mult:
+                g0, g1 = GROUPS[g]
+                nc.tensor.matmul_mx(
+                    out=banks[g][:, 0 : g1 - g0],
+                    lhsT=w_codes[:, b, :].bitcast(FP8X4),
+                    lhsT_scale=w_plane[:, b, :],
+                    rhs=codes[b][:, g0:g1].bitcast(FP8X4),
+                    rhs_scale=planes[b][:, g0:g1],
+                    start=(b == 0),
+                    stop=(b == PASSES - 1),
+                )
+                if b == PASSES - 1:
+                    nc.scalar.copy(out=y[:, g0:g1], in_=banks[g][:, 0 : g1 - g0])
 
         picked = [keep.tile([P, V], F32, name=f"picked{d}") for d in range(D)]
-        sum2 = keep.tile([P, V], F32)
-        sum3 = keep.tile([P, V], F32)
+        scaled = [keep.tile([P, V], F32, name=f"scaled{d}") for d in range(D)]
         result = keep.tile([P, V], F32)
-        H = V // 2
+        partial = keep.tile([P, V], F32)
+        sums = [banks[6][:, 0:H], banks[7][:, 0:H]]
+        turned = {
+            (0, 0): banks[4][:, 0:H],
+            (0, 1): banks[5][:, 0:H],
+            (1, 0): banks[3][:, 0:H],
+            (1, 1): banks[0][:, 0:H],
+        }
 
-        def gather(d, v0, v1):
-            nc.vector.tensor_tensor(picked[d][:, v0:v1], y[:].indirect(lists[d][:, v0 // 16 : v1 // 16]), gates[:, d, v0:v1], MULT)
+        def half(h):
+            return slice(h * H, (h + 1) * H)
 
-        gather(0, 0, V)
-        gather(1, 0, V)
-        gather(2, 0, V)
-        nc.vector.tensor_tensor(sum2[:], picked[0][:], picked[1][:], ADD)
-        gather(3, 0, H)
-        nc.vector.tensor_tensor(sum3[:], sum2[:], picked[2][:], ADD)
-        gather(3, H, V)
-        nc.vector.tensor_tensor(result[:, 0:H], sum3[:, 0:H], picked[3][:, 0:H], ADD)
+        def offsets(d, v0, v1):
+            return y[:].indirect(lists[d][:, v0 // 16 : v1 // 16])
+
+        def fetch(d, v0, v1):
+            nc.vector.tensor_copy(picked[d][:, v0:v1], offsets(d, v0, v1))
+
+        def fetch_gated(d, v0, v1):
+            nc.vector.tensor_tensor(picked[d][:, v0:v1], offsets(d, v0, v1), gates[:, d, v0:v1], MULT)
+
+        def turn(d, h):
+            nc.tensor.transpose(turned[(d, h)], picked[d][:, half(h)], ident[:])
+
+        def scale(d, h):
+            nc.scalar.activation(scaled[d][:, half(h)], turned[(d, h)], COPY, scale=gate_cols[:, 2 * d + h : 2 * d + h + 1])
+
+        def turn_back(d, h, start, stop):
+            nc.tensor.matmul(sums[h], lhsT=scaled[d][:, half(h)], rhs=ident[:], start=start, stop=stop, is_transpose=True)
+
+        fetch(0, 0, V)
+        turn(0, 0)
+        turn(0, 1)
+        fetch(1, 0, V)
+        turn(1, 0)
+        turn(1, 1)
+        scale(0, 0)
+        scale(0, 1)
+        scale(1, 0)
+        scale(1, 1)
+        fetch_gated(2, 0, V)
+        fetch_gated(3, 0, H)
+        fetch_gated(3, H, V)
+        turn_back(0, 0, True, False)
+        turn_back(0, 1, True, False)
+        turn_back(1, 0, False, True)
+        turn_back(1, 1, False, True)
+        nc.vector.tensor_tensor(partial[:, 0:H], picked[2][:, 0:H], picked[3][:, 0:H], ADD)
+        nc.vector.tensor_tensor(partial[:, H:V], picked[2][:, H:V], picked[3][:, H:V], ADD)
+        nc.vector.tensor_tensor(result[:, 0:H], sums[0], partial[:, 0:H], ADD)
         nc.scalar.dma_start(out=out[:, 0:H], in_=result[:, 0:H])
-        nc.vector.tensor_tensor(result[:, H:V], sum3[:, H:V], picked[3][:, H:V], ADD)
+        nc.vector.tensor_tensor(result[:, H:V], sums[1], partial[:, H:V], ADD)
         nc.sync.dma_start(out=out[:, H:V], in_=result[:, H:V])

@@ -41,7 +41,7 @@ def tile_picked_agg_lin_none_sub_l_kernel(tc, xT, w_words, w_scales, gate, pos1,
 
         lists = [keep.tile([P, V // 16], U16, name=f"list{d}") for d in range(D)]
         w_codes = keep.tile([P, PASSES, M], U32, align_bytes=64)
-        w_plane = keep.tile([P, PASSES, M], U8, align_bytes=64)
+        w_plane = keep.tile([P, M], U8, align_bytes=64)
         y = keep.tile([P, T], F32)
         banks = [psum.tile([P, 512], F32, name=f"bank{b}") for b in range(8)]
         w_rows = w_words.rearrange("a p m r -> p a (m r)").bitcast(I32)
@@ -57,17 +57,17 @@ def tile_picked_agg_lin_none_sub_l_kernel(tc, xT, w_words, w_scales, gate, pos1,
         def load_scales(queue):
             for q in range(4):
                 queue.dma_start(
-                    out=w_plane[32 * q : 32 * q + 4, :, :].bitcast(I32),
-                    in_=w_scales[:, 4 * q : 4 * q + 4, :].rearrange("a r m -> r a m").bitcast(I32),
+                    out=w_plane[32 * q : 32 * q + 16, :].bitcast(I32),
+                    in_=w_scales[:, 4 * q : 4 * q + 4, :].bitcast(I32),
                 )
 
         gate_cols = keep.tile([P, 4], F32)
         ident = keep.tile([P, P], F32)
         gates = keep.tile([P, D, V], F32)
         nc.gpsimd.memset(w_plane[:].bitcast(I32), 0)
-        load_scales(nc.gpsimd)
         make_identity(nc, ident[:])
         nc.scalar.dma_start(out=w_codes[:, 0:3, :].bitcast(I32), in_=w_rows[:, 0:3, :])
+        load_scales(nc.scalar)
         raws = [load_x(n) for n in range(len(LOADS))]
         nc.sync.dma_start(out=w_codes[:, 3, :].bitcast(I32), in_=w_rows[:, 3, :])
         nc.sync.dma_start(lists[0][:], pos1)
@@ -103,7 +103,7 @@ def tile_picked_agg_lin_none_sub_l_kernel(tc, xT, w_words, w_scales, gate, pos1,
                 nc.tensor.matmul_mx(
                     out=banks[g][:, 0 : g1 - g0],
                     lhsT=w_codes[:, b, :].bitcast(FP8X4),
-                    lhsT_scale=w_plane[:, b, :],
+                    lhsT_scale=w_plane[4 * b :, :],
                     rhs=codes[b][:, g0:g1].bitcast(FP8X4),
                     rhs_scale=planes[b][:, g0:g1],
                     start=(b == 0),

@@ -24,12 +24,12 @@ PASSES = K // K_PASS
 H = V // 2
 GROUPS = ((0, 256), (256, 384), (384, 512))
 LOADS = (
-    (0, 0, 4, 0, 512, ((0, 256), (256, 320)), ((320, 512),), ((0, 256), (256, 512)), ((0, 0), (0, 1), (0, 2))),
-    (1, 0, 4, 0, 512, ((0, 256), (256, 320)), ((320, 512),), ((0, 256), (256, 512)), ((1, 0), (1, 1), (1, 2))),
-    (2, 0, 4, 0, 512, ((0, 256), (256, 320)), ((320, 512),), ((0, 256), (256, 512)), ((2, 0), (2, 1), (2, 2))),
-    (3, 0, 4, 0, 256, ((0, 168),), ((168, 256),), ((0, 256),), ((3, 0),)),
-    (3, 0, 4, 256, 384, ((256, 340),), ((340, 384),), ((256, 384),), ((3, 1),)),
-    (3, 0, 4, 384, 512, ((384, 468),), ((468, 512),), ((384, 512),), ((3, 2),)),
+    (0, 0, 4, 0, 512, ((0, 256), (256, 288)), ((288, 512),), ((0, 256), (256, 512)), ((0, 0), (0, 1), (0, 2))),
+    (1, 0, 4, 0, 512, ((0, 256), (256, 288)), ((288, 512),), ((0, 256), (256, 512)), ((1, 0), (1, 1), (1, 2))),
+    (2, 0, 4, 0, 512, ((0, 256), (256, 288)), ((288, 512),), ((0, 256), (256, 512)), ((2, 0), (2, 1), (2, 2))),
+    (3, 0, 4, 0, 256, ((0, 128), (128, 144)), ((144, 256),), ((0, 128), (128, 256)), ((3, 0),)),
+    (3, 0, 4, 256, 384, ((256, 328),), ((328, 384),), ((256, 384),), ((3, 1),)),
+    (3, 0, 4, 384, 512, ((384, 448), (448, 480)), ((480, 512),), ((384, 448), (448, 512)), ((3, 2),)),
 )
 
 
@@ -84,13 +84,13 @@ def tile_picked_agg_lin_none_sub_l_kernel(tc, xT, w_words, w_scales, gate, pos1,
         for raw, (a, j0, j1, lo, hi, vec, sca, quant, mult) in zip(raws, LOADS):
             for c0, c1 in sca:
                 nc.scalar.copy(
-                    out=grouped[a][:, c0:c1, j0:j1],
-                    in_=raw[:, :, c0 - lo : c1 - lo].rearrange("p j c -> p c j"),
+                    out=grouped[a][:, c0:c1, j0:j1].rearrange("p (c i) j -> p c j i", i=4),
+                    in_=raw[:, :, c0 - lo : c1 - lo].rearrange("p j (c i) -> p c j i", i=4),
                 )
             for c0, c1 in vec:
                 nc.vector.tensor_copy(
-                    out=grouped[a][:, c0:c1, j0:j1],
-                    in_=raw[:, :, c0 - lo : c1 - lo].rearrange("p j c -> p c j"),
+                    out=grouped[a][:, c0:c1, j0:j1].rearrange("p (c i) j -> p c j i", i=4),
+                    in_=raw[:, :, c0 - lo : c1 - lo].rearrange("p j (c i) -> p c j i", i=4),
                 )
             for c0, c1 in quant:
                 nc.vector.quantize_mx(

@@ -21,15 +21,18 @@ P = 128
 PACK = 4
 K_PASS = P * PACK
 PASSES = K // K_PASS
+LAST = PASSES - 1
 H = V // 2
+RUN = 4
+TURNED = 2
+
 GROUPS = ((0, 256), (256, 384), (384, 512))
-LOADS = (
-    (0, 0, 4, 0, 512, ((0, 256), (256, 288)), ((288, 512),), ((0, 256), (256, 512)), ((0, 0), (0, 1), (0, 2))),
-    (1, 0, 4, 0, 512, ((0, 256), (256, 288)), ((288, 512),), ((0, 256), (256, 512)), ((1, 0), (1, 1), (1, 2))),
-    (2, 0, 4, 0, 512, ((0, 256), (256, 288)), ((288, 512),), ((0, 256), (256, 512)), ((2, 0), (2, 1), (2, 2))),
-    (3, 0, 4, 0, 256, ((0, 128), (128, 144)), ((144, 256),), ((0, 128), (128, 256)), ((3, 0),)),
-    (3, 0, 4, 256, 384, ((256, 328),), ((328, 384),), ((256, 384),), ((3, 1),)),
-    (3, 0, 4, 384, 512, ((384, 448), (448, 480)), ((480, 512),), ((384, 448), (448, 512)), ((3, 2),)),
+
+WHOLE = ((0, T), ((0, 256), (256, 288)), (288, T), ((0, 256), (256, T)), (0, 1, 2))
+LOADS = tuple((a,) + WHOLE for a in range(LAST)) + (
+    (LAST, (0, 256), ((0, 128), (128, 144)), (144, 256), ((0, 128), (128, 256)), (0,)),
+    (LAST, (256, 384), ((256, 328),), (328, 384), ((256, 384),), (1,)),
+    (LAST, (384, 512), ((384, 448), (448, 480)), (480, 512), ((384, 448), (448, 512)), (2,)),
 )
 
 
@@ -41,130 +44,120 @@ def tile_picked_agg_lin_none_sub_l_kernel(tc, xT, w_words, w_scales, gate, pos1,
 
         lists = [keep.tile([P, V // 16], U16, name=f"list{d}") for d in range(D)]
         w_codes = keep.tile([P, PASSES, M], U32, align_bytes=64)
-        w_plane = keep.tile([P, M], U8, align_bytes=64)
+        w_scale_rows = keep.tile([P, M], U8, align_bytes=64)
         y = keep.tile([P, T], F32)
         banks = [psum.tile([P, 512], F32, name=f"bank{b}") for b in range(8)]
         w_rows = w_words.rearrange("a p m r -> p a (m r)").bitcast(I32)
-        gate_rows = gate.rearrange("d m v -> m d v")
 
         def load_x(n):
-            a, j0, j1, lo, hi = LOADS[n][0:5]
+            a, (lo, hi) = LOADS[n][0:2]
             rows = xT[a * K_PASS : (a + 1) * K_PASS, :].rearrange("(p j) t -> p j t", j=PACK)
-            raw = keep.tile([P, j1 - j0, hi - lo], F32, name=f"raw{n}")
-            nc.sync.dma_start(out=raw[:], in_=rows[:, j0:j1, lo:hi])
+            raw = keep.tile([P, PACK, hi - lo], F32, name=f"raw{n}")
+            nc.sync.dma_start(out=raw[:], in_=rows[:, :, lo:hi])
             return raw
 
-        def load_scales(queue):
-            for q in range(4):
-                queue.dma_start(
-                    out=w_plane[32 * q : 32 * q + 16, :].bitcast(I32),
-                    in_=w_scales[:, 4 * q : 4 * q + 4, :].bitcast(I32),
-                )
+        def load_w(queue, passes):
+            queue.dma_start(out=w_codes[:, passes, :].bitcast(I32), in_=w_rows[:, passes, :])
 
-        gate_cols = keep.tile([P, 4], F32)
+        gate_cols = keep.tile([P, 2 * TURNED], F32)
         ident = keep.tile([P, P], F32)
-        gates = keep.tile([P, D, V], F32)
-        nc.gpsimd.memset(w_plane[:].bitcast(I32), 0)
+        gates = keep.tile([P, D - TURNED, V], F32)
+
+        nc.gpsimd.memset(w_scale_rows[:].bitcast(I32), 0)
         make_identity(nc, ident[:])
-        nc.scalar.dma_start(out=w_codes[:, 0:3, :].bitcast(I32), in_=w_rows[:, 0:3, :])
-        load_scales(nc.scalar)
-        raws = [load_x(n) for n in range(len(LOADS))]
-        nc.sync.dma_start(out=w_codes[:, 3, :].bitcast(I32), in_=w_rows[:, 3, :])
+
+        load_w(nc.scalar, 0)
+        for q in range(4):
+            nc.scalar.dma_start(
+                out=w_scale_rows[32 * q : 32 * q + 16, :].bitcast(I32),
+                in_=w_scales[:, 4 * q : 4 * q + 4, :].bitcast(I32),
+            )
+
+        raws = []
+        for n in range(len(LOADS)):
+            raws.append(load_x(n))
+            if n + 1 < LAST:
+                load_w(nc.sync, n + 1)
+        load_w(nc.sync, LAST)
         nc.sync.dma_start(lists[0][:], pos1)
         nc.sync.dma_start(lists[1][:], pos2)
+        half_rows = gate.rearrange("d m (h p) -> (d m h) p", h=2)
         with nc.allow_non_contiguous_dma(reason="one gate value a partition"):
-            nc.sync.dma_start(out=gate_cols[:], in_=gate.rearrange("d m (h p) -> (d m h) p", h=2)[0 : 4 * 129 : 129, :].rearrange("i p -> p i"))
+            nc.sync.dma_start(out=gate_cols[:], in_=half_rows[0 : 2 * TURNED * 129 : 129, :].rearrange("i p -> p i"))
         nc.sync.dma_start(lists[2][:], pos3)
-        nc.sync.dma_start(out=gates[:, 2:4, :], in_=gate_rows[:, 2:4, :])
+        nc.sync.dma_start(out=gates[:], in_=gate.rearrange("d m v -> m d v")[:, TURNED:D, :])
         nc.sync.dma_start(lists[3][:], pos4)
 
         grouped = [keep.tile([P, T, PACK], BF16, align_bytes=64, name=f"grouped{a}") for a in range(PASSES)]
-        codes = [keep.tile([P, T], U32, align_bytes=64, name=f"codes{a}") for a in range(PASSES)]
-        planes = [keep.tile([P, T], U8, align_bytes=64, name=f"plane{a}") for a in range(PASSES)]
-        for raw, (a, j0, j1, lo, hi, vec, sca, quant, mult) in zip(raws, LOADS):
-            for c0, c1 in sca:
-                nc.scalar.copy(
-                    out=grouped[a][:, c0:c1, j0:j1].rearrange("p (c i) j -> p c j i", i=4),
-                    in_=raw[:, :, c0 - lo : c1 - lo].rearrange("p j (c i) -> p c j i", i=4),
-                )
-            for c0, c1 in vec:
-                nc.vector.tensor_copy(
-                    out=grouped[a][:, c0:c1, j0:j1].rearrange("p (c i) j -> p c j i", i=4),
-                    in_=raw[:, :, c0 - lo : c1 - lo].rearrange("p j (c i) -> p c j i", i=4),
-                )
-            for c0, c1 in quant:
+        x_codes = [keep.tile([P, T], U32, align_bytes=64, name=f"x_codes{a}") for a in range(PASSES)]
+        x_scales = [keep.tile([P, T], U8, align_bytes=64, name=f"x_scales{a}") for a in range(PASSES)]
+
+        def interleave(copy, raw, a, lo, c0, c1):
+            copy(
+                out=grouped[a][:, c0:c1, :].rearrange("p (c i) j -> p c j i", i=RUN),
+                in_=raw[:, :, c0 - lo : c1 - lo].rearrange("p j (c i) -> p c j i", i=RUN),
+            )
+
+        for raw, (a, (lo, hi), on_vector, on_scalar, quantised, groups) in zip(raws, LOADS):
+            interleave(nc.scalar.copy, raw, a, lo, *on_scalar)
+            for c0, c1 in on_vector:
+                interleave(nc.vector.tensor_copy, raw, a, lo, c0, c1)
+            for c0, c1 in quantised:
                 nc.vector.quantize_mx(
-                    out=codes[a][:, c0:c1].bitcast(FP8X4),
-                    scales=planes[a][:, c0:c1],
+                    out=x_codes[a][:, c0:c1].bitcast(FP8X4),
+                    scales=x_scales[a][:, c0:c1],
                     in_=grouped[a][:, c0:c1, :].rearrange("p c j -> p (c j)"),
                 )
-            for b, g in mult:
+            for g in groups:
                 g0, g1 = GROUPS[g]
                 nc.tensor.matmul_mx(
                     out=banks[g][:, 0 : g1 - g0],
-                    lhsT=w_codes[:, b, :].bitcast(FP8X4),
-                    lhsT_scale=w_plane[4 * b :, :],
-                    rhs=codes[b][:, g0:g1].bitcast(FP8X4),
-                    rhs_scale=planes[b][:, g0:g1],
-                    start=(b == 0),
-                    stop=(b == PASSES - 1),
+                    lhsT=w_codes[:, a, :].bitcast(FP8X4),
+                    lhsT_scale=w_scale_rows[4 * a :, :],
+                    rhs=x_codes[a][:, g0:g1].bitcast(FP8X4),
+                    rhs_scale=x_scales[a][:, g0:g1],
+                    start=(a == 0),
+                    stop=(a == LAST),
                 )
-                if b == PASSES - 1:
+                if a == LAST:
                     nc.scalar.copy(out=y[:, g0:g1], in_=banks[g][:, 0 : g1 - g0])
 
         picked = [keep.tile([P, V], F32, name=f"picked{d}") for d in range(D)]
-        scaled = [keep.tile([P, V], F32, name=f"scaled{d}") for d in range(D)]
+        scaled = [keep.tile([P, V], F32, name=f"scaled{d}") for d in range(TURNED)]
         result = keep.tile([P, V], F32)
-        partial = keep.tile([P, V], F32)
-        sums = [banks[6][:, 0:H], banks[7][:, 0:H]]
-        turned = {
-            (0, 0): banks[4][:, 0:H],
-            (0, 1): banks[5][:, 0:H],
-            (1, 0): banks[3][:, 0:H],
-            (1, 1): banks[0][:, 0:H],
-        }
+        fused_sum = keep.tile([P, V], F32)
+        turned_sum = [banks[6][:, 0:H], banks[7][:, 0:H]]
+        turned = [[banks[4][:, 0:H], banks[5][:, 0:H]], [banks[3][:, 0:H], banks[0][:, 0:H]]]
+        halves = [slice(0, H), slice(H, V)]
 
-        def half(h):
-            return slice(h * H, (h + 1) * H)
-
-        def offsets(d, v0, v1):
+        def neighbours(d, v0, v1):
             return y[:].indirect(lists[d][:, v0 // 16 : v1 // 16])
 
-        def fetch(d, v0, v1):
-            nc.vector.tensor_copy(picked[d][:, v0:v1], offsets(d, v0, v1))
+        def gather_gated(d, v0, v1):
+            nc.vector.tensor_tensor(picked[d][:, v0:v1], neighbours(d, v0, v1), gates[:, d - TURNED, v0:v1], MULT)
 
-        def fetch_gated(d, v0, v1):
-            nc.vector.tensor_tensor(picked[d][:, v0:v1], offsets(d, v0, v1), gates[:, d, v0:v1], MULT)
-
-        def turn(d, h):
-            nc.tensor.transpose(turned[(d, h)], picked[d][:, half(h)], ident[:])
-
-        def scale(d, h):
-            nc.scalar.activation(scaled[d][:, half(h)], turned[(d, h)], COPY, scale=gate_cols[:, 2 * d + h : 2 * d + h + 1])
-
-        def turn_back(d, h, start, stop):
-            nc.tensor.matmul(sums[h], lhsT=scaled[d][:, half(h)], rhs=ident[:], start=start, stop=stop, is_transpose=True)
-
-        fetch(0, 0, V)
-        turn(0, 0)
-        turn(0, 1)
-        fetch(1, 0, V)
-        turn(1, 0)
-        turn(1, 1)
-        scale(0, 0)
-        scale(0, 1)
-        scale(1, 0)
-        scale(1, 1)
-        fetch_gated(2, 0, V)
-        fetch_gated(3, 0, H)
-        fetch_gated(3, H, V)
-        turn_back(0, 0, True, False)
-        turn_back(0, 1, True, False)
-        turn_back(1, 0, False, True)
-        turn_back(1, 1, False, True)
-        nc.vector.tensor_tensor(partial[:, 0:H], picked[2][:, 0:H], picked[3][:, 0:H], ADD)
-        nc.vector.tensor_tensor(partial[:, H:V], picked[2][:, H:V], picked[3][:, H:V], ADD)
-        nc.vector.tensor_tensor(result[:, 0:H], sums[0], partial[:, 0:H], ADD)
-        nc.scalar.dma_start(out=out[:, 0:H], in_=result[:, 0:H])
-        nc.vector.tensor_tensor(result[:, H:V], sums[1], partial[:, H:V], ADD)
-        nc.sync.dma_start(out=out[:, H:V], in_=result[:, H:V])
+        for d in range(TURNED):
+            nc.vector.tensor_copy(picked[d][:], neighbours(d, 0, V))
+            for h in range(2):
+                nc.tensor.transpose(turned[d][h], picked[d][:, halves[h]], ident[:])
+        for d in range(TURNED):
+            for h in range(2):
+                nc.scalar.activation(scaled[d][:, halves[h]], turned[d][h], COPY, scale=gate_cols[:, 2 * d + h : 2 * d + h + 1])
+        gather_gated(2, 0, V)
+        gather_gated(3, 0, H)
+        gather_gated(3, H, V)
+        for d in range(TURNED):
+            for h in range(2):
+                nc.tensor.matmul(
+                    turned_sum[h],
+                    lhsT=scaled[d][:, halves[h]],
+                    rhs=ident[:],
+                    start=(d == 0),
+                    stop=(d == TURNED - 1),
+                    is_transpose=True,
+                )
+        for h in range(2):
+            nc.vector.tensor_tensor(fused_sum[:, halves[h]], picked[2][:, halves[h]], picked[3][:, halves[h]], ADD)
+        for h, queue in enumerate((nc.scalar, nc.sync)):
+            nc.vector.tensor_tensor(result[:, halves[h]], turned_sum[h], fused_sum[:, halves[h]], ADD)
+            queue.dma_start(out=out[:, halves[h]], in_=result[:, halves[h]])

@@ -15,7 +15,6 @@ U8 = mybir.dt.uint8
 FP8X4 = mybir.dt.float8_e4m3fn_x4
 MULT = mybir.AluOpType.mult
 ADD = mybir.AluOpType.add
-COPY = mybir.ActivationFunctionType.Copy
 
 P = 128
 PACK = 4
@@ -28,11 +27,11 @@ TURNED = 2
 
 GROUPS = ((0, 256), (256, 384), (384, 512))
 
-WHOLE = ((0, T), ((0, 256), (256, 288)), (288, T), ((0, 256), (256, T)), (0, 1, 2))
+WHOLE = ((0, T), ((0, 128), (128, 256)), (256, T), ((0, 128), (128, 256), (256, T)), (0, 1, 2))
 LOADS = tuple((a,) + WHOLE for a in range(LAST)) + (
-    (LAST, (0, 256), ((0, 128), (128, 144)), (144, 256), ((0, 128), (128, 256)), (0,)),
-    (LAST, (256, 384), ((256, 328),), (328, 384), ((256, 384),), (1,)),
-    (LAST, (384, 512), ((384, 448), (448, 480)), (480, 512), ((384, 448), (448, 512)), (2,)),
+    (LAST, (0, 256), ((0, 64), (64, 128)), (128, 256), ((0, 64), (64, 128), (128, 256)), (0,)),
+    (LAST, (256, 384), (), (256, 384), ((256, 384),), (1,)),
+    (LAST, (384, 512), ((384, 448),), (448, 512), ((384, 448), (448, 512)), (2,)),
 )
 
 
@@ -59,9 +58,8 @@ def tile_picked_agg_lin_none_sub_l_kernel(tc, xT, w_words, w_scales, gate, pos1,
         def load_w(queue, passes):
             queue.dma_start(out=w_codes[:, passes, :].bitcast(I32), in_=w_rows[:, passes, :])
 
-        gate_cols = keep.tile([P, 2 * TURNED], F32)
         ident = keep.tile([P, P], F32)
-        gates = keep.tile([P, D - TURNED, V], F32)
+        gates = [keep.tile([P, V], F32, name=f"gates{d}") for d in range(D)]
 
         nc.gpsimd.memset(w_scale_rows[:].bitcast(I32), 0)
         make_identity(nc, ident[:])
@@ -79,14 +77,9 @@ def tile_picked_agg_lin_none_sub_l_kernel(tc, xT, w_words, w_scales, gate, pos1,
             if n + 1 < LAST:
                 load_w(nc.sync, n + 1)
         load_w(nc.sync, LAST)
-        nc.sync.dma_start(lists[0][:], pos1)
-        nc.sync.dma_start(lists[1][:], pos2)
-        half_rows = gate.rearrange("d m (h p) -> (d m h) p", h=2)
-        with nc.allow_non_contiguous_dma(reason="one gate value a partition"):
-            nc.sync.dma_start(out=gate_cols[:], in_=half_rows[0 : 2 * TURNED * 129 : 129, :].rearrange("i p -> p i"))
-        nc.sync.dma_start(lists[2][:], pos3)
-        nc.sync.dma_start(out=gates[:], in_=gate.rearrange("d m v -> m d v")[:, TURNED:D, :])
-        nc.sync.dma_start(lists[3][:], pos4)
+        for d, pos in enumerate((pos1, pos2, pos3, pos4)):
+            nc.sync.dma_start(lists[d][:], pos)
+            nc.sync.dma_start(out=gates[d][:], in_=gate[d])
 
         grouped = [keep.tile([P, T, PACK], BF16, align_bytes=64, name=f"grouped{a}") for a in range(PASSES)]
         x_codes = [keep.tile([P, T], U32, align_bytes=64, name=f"x_codes{a}") for a in range(PASSES)]
@@ -123,41 +116,36 @@ def tile_picked_agg_lin_none_sub_l_kernel(tc, xT, w_words, w_scales, gate, pos1,
                     nc.scalar.copy(out=y[:, g0:g1], in_=banks[g][:, 0 : g1 - g0])
 
         picked = [keep.tile([P, V], F32, name=f"picked{d}") for d in range(D)]
-        scaled = [keep.tile([P, V], F32, name=f"scaled{d}") for d in range(TURNED)]
+        turned_copy = keep.tile([P, V], F32)
         result = keep.tile([P, V], F32)
         fused_sum = keep.tile([P, V], F32)
-        turned_sum = [banks[6][:, 0:H], banks[7][:, 0:H]]
-        turned = [[banks[4][:, 0:H], banks[5][:, 0:H]], [banks[3][:, 0:H], banks[0][:, 0:H]]]
+        turned = [banks[4][:, 0:H], banks[5][:, 0:H]]
+        turned_back = [banks[6][:, 0:H], banks[7][:, 0:H]]
         halves = [slice(0, H), slice(H, V)]
 
-        def neighbours(d, v0, v1):
-            return y[:].indirect(lists[d][:, v0 // 16 : v1 // 16])
-
         def gather_gated(d, v0, v1):
-            nc.vector.tensor_tensor(picked[d][:, v0:v1], neighbours(d, v0, v1), gates[:, d - TURNED, v0:v1], MULT)
+            neighbours = y[:].indirect(lists[d][:, v0 // 16 : v1 // 16])
+            nc.vector.tensor_tensor(picked[d][:, v0:v1], neighbours, gates[d][:, v0:v1], MULT)
 
         for d in range(TURNED):
-            nc.vector.tensor_copy(picked[d][:], neighbours(d, 0, V))
-            for h in range(2):
-                nc.tensor.transpose(turned[d][h], picked[d][:, halves[h]], ident[:])
-        for d in range(TURNED):
-            for h in range(2):
-                nc.scalar.activation(scaled[d][:, halves[h]], turned[d][h], COPY, scale=gate_cols[:, 2 * d + h : 2 * d + h + 1])
-        gather_gated(2, 0, V)
-        gather_gated(3, 0, H)
-        gather_gated(3, H, V)
-        for d in range(TURNED):
+            gather_gated(d, 0, V)
             for h in range(2):
                 nc.tensor.matmul(
-                    turned_sum[h],
-                    lhsT=scaled[d][:, halves[h]],
+                    turned[h],
+                    lhsT=picked[d][:, halves[h]],
                     rhs=ident[:],
                     start=(d == 0),
                     stop=(d == TURNED - 1),
                     is_transpose=True,
                 )
         for h in range(2):
+            nc.scalar.copy(out=turned_copy[:, halves[h]], in_=turned[h])
+            nc.tensor.transpose(turned_back[h], turned_copy[:, halves[h]], ident[:])
+        gather_gated(2, 0, V)
+        gather_gated(3, 0, H)
+        gather_gated(3, H, V)
+        for h in range(2):
             nc.vector.tensor_tensor(fused_sum[:, halves[h]], picked[2][:, halves[h]], picked[3][:, halves[h]], ADD)
         for h, queue in enumerate((nc.scalar, nc.sync)):
-            nc.vector.tensor_tensor(result[:, halves[h]], turned_sum[h], fused_sum[:, halves[h]], ADD)
+            nc.vector.tensor_tensor(result[:, halves[h]], turned_back[h], fused_sum[:, halves[h]], ADD)
             queue.dma_start(out=out[:, halves[h]], in_=result[:, halves[h]])

@@ -65,15 +65,16 @@ def tile_picked_agg_lin_none_sub_l_kernel(tc, xT, w_words, w_scales, gate, pos1,
         make_identity(nc, ident[:])
 
         load_w(nc.scalar, 0)
-        for q in range(4):
-            nc.scalar.dma_start(
-                out=w_scale_rows[32 * q : 32 * q + 16, :].bitcast(I32),
-                in_=w_scales[:, 4 * q : 4 * q + 4, :].bitcast(I32),
-            )
 
         raws = []
         for n in range(len(LOADS)):
             raws.append(load_x(n))
+            if n == 0:
+                for q in range(4):
+                    nc.sync.dma_start(
+                        out=w_scale_rows[32 * q : 32 * q + 16, :].bitcast(I32),
+                        in_=w_scales[:, 4 * q : 4 * q + 4, :].bitcast(I32),
+                    )
             if n + 1 < LAST:
                 load_w(nc.sync, n + 1)
         load_w(nc.sync, LAST)

@@ -1,7 +1,6 @@
 from contextlib import ExitStack
 
 import concourse.mybir as mybir
-from concourse.masks import make_identity
 
 K, T, D, V, M = 2048, 512, 4, 256, 128
 FLOPS = 2 * K * M * T + 2 * D * M * V
@@ -15,23 +14,26 @@ U8 = mybir.dt.uint8
 FP8X4 = mybir.dt.float8_e4m3fn_x4
 MULT = mybir.AluOpType.mult
 ADD = mybir.AluOpType.add
+COPY = mybir.ActivationFunctionType.Copy
 
 P = 128
 PACK = 4
 K_PASS = P * PACK
 PASSES = K // K_PASS
 LAST = PASSES - 1
-H = V // 2
 RUN = 4
-TURNED = 2
+H = V // 2
+FUSED = 64
 
 GROUPS = ((0, 256), (256, 384), (384, 512))
 
-WHOLE = ((0, T), ((0, 128), (128, 256)), (256, T), ((0, 128), (128, 256), (256, T)), (0, 1, 2))
-LOADS = tuple((a,) + WHOLE for a in range(LAST)) + (
-    (LAST, (0, 256), ((0, 64), (64, 128)), (128, 256), ((0, 64), (64, 128), (128, 256)), (0,)),
-    (LAST, (256, 384), (), (256, 384), ((256, 384),), (1,)),
-    (LAST, (384, 512), ((384, 448),), (448, 512), ((384, 448), (448, 512)), (2,)),
+ALL = (0, T)
+LOADS = tuple(
+    (a, (0, 4), ALL, ((0, 128), (128, 256)), (256, T), ((0, 128), (128, 256), (256, T)), (0, 1, 2)) for a in range(LAST)
+) + (
+    (LAST, (0, 4), (0, 256), ((0, 64), (64, 128)), (128, 256), ((0, 64), (64, 128), (128, 256)), (0,)),
+    (LAST, (0, 4), (256, 384), (), (256, 384), ((256, 384),), (1,)),
+    (LAST, (0, 4), (384, 512), ((384, 448),), (448, 512), ((384, 448), (448, 512)), (2,)),
 )
 
 
@@ -42,27 +44,25 @@ def tile_picked_agg_lin_none_sub_l_kernel(tc, xT, w_words, w_scales, gate, pos1,
         psum = ctx.enter_context(tc.psum_pool(name="psum", bufs=1))
 
         lists = [keep.tile([P, V // 16], U16, name=f"list{d}") for d in range(D)]
+        gates = [keep.tile([P, V], F32, name=f"gates{d}") for d in range(D)]
         w_codes = keep.tile([P, PASSES, M], U32, align_bytes=64)
         w_scale_rows = keep.tile([P, M], U8, align_bytes=64)
         y = keep.tile([P, T], F32)
-        banks = [psum.tile([P, 512], F32, name=f"bank{b}") for b in range(8)]
+        banks = [psum.tile([P, 512], F32, name=f"bank{g}") for g in range(len(GROUPS))]
         w_rows = w_words.rearrange("a p m r -> p a (m r)").bitcast(I32)
+        positions = (pos1, pos2, pos3, pos4)
 
         def load_x(n):
-            a, (lo, hi) = LOADS[n][0:2]
+            a, (j0, j1), (lo, hi) = LOADS[n][0:3]
             rows = xT[a * K_PASS : (a + 1) * K_PASS, :].rearrange("(p j) t -> p j t", j=PACK)
-            raw = keep.tile([P, PACK, hi - lo], F32, name=f"raw{n}")
-            nc.sync.dma_start(out=raw[:], in_=rows[:, :, lo:hi])
+            raw = keep.tile([P, j1 - j0, hi - lo], F32, name=f"raw{n}")
+            nc.sync.dma_start(out=raw[:], in_=rows[:, j0:j1, lo:hi])
             return raw
 
-        def load_w(queue, passes):
-            queue.dma_start(out=w_codes[:, passes, :].bitcast(I32), in_=w_rows[:, passes, :])
-
-        ident = keep.tile([P, P], F32)
-        gates = [keep.tile([P, V], F32, name=f"gates{d}") for d in range(D)]
+        def load_w(queue, a):
+            queue.dma_start(out=w_codes[:, a, :].bitcast(I32), in_=w_rows[:, a, :])
 
         nc.gpsimd.memset(w_scale_rows[:].bitcast(I32), 0)
-        make_identity(nc, ident[:])
 
         load_w(nc.scalar, 0)
 
@@ -78,24 +78,28 @@ def tile_picked_agg_lin_none_sub_l_kernel(tc, xT, w_words, w_scales, gate, pos1,
             if n + 1 < LAST:
                 load_w(nc.sync, n + 1)
         load_w(nc.sync, LAST)
-        for d, pos in enumerate((pos1, pos2, pos3, pos4)):
-            nc.sync.dma_start(lists[d][:], pos)
+        nc.sync.dma_start(lists[3][:], positions[3])
+        nc.sync.dma_start(lists[0][:], positions[0])
+        nc.sync.dma_start(out=gates[3][:], in_=gate[3])
+        nc.sync.dma_start(lists[2][:], positions[2])
+        nc.sync.dma_start(lists[1][:], positions[1])
+        for d in (0, 2, 1):
             nc.sync.dma_start(out=gates[d][:], in_=gate[d])
 
         grouped = [keep.tile([P, T, PACK], BF16, align_bytes=64, name=f"grouped{a}") for a in range(PASSES)]
         x_codes = [keep.tile([P, T], U32, align_bytes=64, name=f"x_codes{a}") for a in range(PASSES)]
         x_scales = [keep.tile([P, T], U8, align_bytes=64, name=f"x_scales{a}") for a in range(PASSES)]
 
-        def interleave(copy, raw, a, lo, c0, c1):
+        def interleave(copy, raw, a, j0, j1, lo, c0, c1):
             copy(
-                out=grouped[a][:, c0:c1, :].rearrange("p (c i) j -> p c j i", i=RUN),
+                out=grouped[a][:, c0:c1, j0:j1].rearrange("p (c i) j -> p c j i", i=RUN),
                 in_=raw[:, :, c0 - lo : c1 - lo].rearrange("p j (c i) -> p c j i", i=RUN),
             )
 
-        for raw, (a, (lo, hi), on_vector, on_scalar, quantised, groups) in zip(raws, LOADS):
-            interleave(nc.scalar.copy, raw, a, lo, *on_scalar)
+        for raw, (a, (j0, j1), (lo, hi), on_vector, on_scalar, quantised, groups) in zip(raws, LOADS):
+            interleave(nc.scalar.copy, raw, a, j0, j1, lo, *on_scalar)
             for c0, c1 in on_vector:
-                interleave(nc.vector.tensor_copy, raw, a, lo, c0, c1)
+                interleave(nc.vector.tensor_copy, raw, a, j0, j1, lo, c0, c1)
             for c0, c1 in quantised:
                 nc.vector.quantize_mx(
                     out=x_codes[a][:, c0:c1].bitcast(FP8X4),
@@ -116,37 +120,45 @@ def tile_picked_agg_lin_none_sub_l_kernel(tc, xT, w_words, w_scales, gate, pos1,
                 if a == LAST:
                     nc.scalar.copy(out=y[:, g0:g1], in_=banks[g][:, 0 : g1 - g0])
 
-        picked = [keep.tile([P, V], F32, name=f"picked{d}") for d in range(D)]
-        turned_copy = keep.tile([P, V], F32)
-        result = keep.tile([P, V], F32)
-        fused_sum = keep.tile([P, V], F32)
-        turned = [banks[4][:, 0:H], banks[5][:, 0:H]]
-        turned_back = [banks[6][:, 0:H], banks[7][:, 0:H]]
-        halves = [slice(0, H), slice(H, V)]
+        plain = [keep.tile([P, V], F32, name=f"plain{d}") for d in range(D - 1)]
+        gated = [keep.tile([P, V], F32, name=f"gated{d}") for d in range(D)]
+        sums = [keep.tile([P, V], F32, name=f"sum{d}") for d in range(D - 1)]
+
+        def neighbours(d, v0, v1):
+            return y[:].indirect(lists[d][:, v0 // 16 : v1 // 16])
+
+        def gather_plain(d, v0, v1):
+            nc.scalar.activation(plain[d][:, v0:v1], neighbours(d, v0, v1), COPY)
 
         def gather_gated(d, v0, v1):
-            neighbours = y[:].indirect(lists[d][:, v0 // 16 : v1 // 16])
-            nc.vector.tensor_tensor(picked[d][:, v0:v1], neighbours, gates[d][:, v0:v1], MULT)
+            nc.vector.tensor_tensor(gated[d][:, v0:v1], neighbours(d, v0, v1), gates[d][:, v0:v1], MULT)
 
-        for d in range(TURNED):
-            gather_gated(d, 0, V)
-            for h in range(2):
-                nc.tensor.matmul(
-                    turned[h],
-                    lhsT=picked[d][:, halves[h]],
-                    rhs=ident[:],
-                    start=(d == 0),
-                    stop=(d == TURNED - 1),
-                    is_transpose=True,
-                )
-        for h in range(2):
-            nc.scalar.copy(out=turned_copy[:, halves[h]], in_=turned[h])
-            nc.tensor.transpose(turned_back[h], turned_copy[:, halves[h]], ident[:])
-        gather_gated(2, 0, V)
-        gather_gated(3, 0, H)
-        gather_gated(3, H, V)
-        for h in range(2):
-            nc.vector.tensor_tensor(fused_sum[:, halves[h]], picked[2][:, halves[h]], picked[3][:, halves[h]], ADD)
-        for h, queue in enumerate((nc.scalar, nc.sync)):
-            nc.vector.tensor_tensor(result[:, halves[h]], turned_back[h], fused_sum[:, halves[h]], ADD)
-            queue.dma_start(out=out[:, halves[h]], in_=result[:, halves[h]])
+        def multiply(d, v0, v1):
+            nc.vector.tensor_tensor(gated[d][:, v0:v1], plain[d][:, v0:v1], gates[d][:, v0:v1], MULT)
+
+        def add(d, v0, v1):
+            so_far = gated[3] if d == 0 else sums[d - 1]
+            nc.vector.tensor_tensor(sums[d][:, v0:v1], so_far[:, v0:v1], gated[d][:, v0:v1], ADD)
+
+        for d in range(2):
+            gather_plain(d, 0, H)
+            gather_plain(d, H, V)
+        gather_plain(2, FUSED, V - FUSED)
+        gather_plain(2, V - FUSED, V)
+
+        gather_gated(3, 0, V)
+        multiply(0, 0, H)
+        gather_gated(2, 0, FUSED)
+        multiply(0, H, V)
+        add(0, 0, H)
+        multiply(1, 0, H)
+        add(0, H, V)
+        multiply(1, H, V)
+        add(1, 0, H)
+        multiply(2, FUSED, V - FUSED)
+        multiply(2, V - FUSED, V)
+        add(1, H, V)
+        add(2, 0, H)
+        nc.scalar.dma_start(out=out[:, 0:H], in_=sums[2][:, 0:H])
+        add(2, H, V)
+        nc.sync.dma_start(out=out[:, H:V], in_=sums[2][:, H:V])

@@ -23,7 +23,6 @@ PASSES = K // K_PASS
 LAST = PASSES - 1
 RUN = 4
 H = V // 2
-FUSED = 64
 
 GROUPS = ((0, 256), (256, 384), (384, 512))
 
@@ -81,9 +80,9 @@ def tile_picked_agg_lin_none_sub_l_kernel(tc, xT, w_words, w_scales, gate, pos1,
         nc.sync.dma_start(lists[3][:], positions[3])
         nc.sync.dma_start(lists[0][:], positions[0])
         nc.sync.dma_start(out=gates[3][:], in_=gate[3])
-        nc.sync.dma_start(lists[2][:], positions[2])
         nc.sync.dma_start(lists[1][:], positions[1])
-        for d in (0, 2, 1):
+        nc.sync.dma_start(lists[2][:], positions[2])
+        for d in range(3):
             nc.sync.dma_start(out=gates[d][:], in_=gate[d])
 
         grouped = [keep.tile([P, T, PACK], BF16, align_bytes=64, name=f"grouped{a}") for a in range(PASSES)]
@@ -140,24 +139,18 @@ def tile_picked_agg_lin_none_sub_l_kernel(tc, xT, w_words, w_scales, gate, pos1,
             so_far = gated[3] if d == 0 else sums[d - 1]
             nc.vector.tensor_tensor(sums[d][:, v0:v1], so_far[:, v0:v1], gated[d][:, v0:v1], ADD)
 
-        for d in range(2):
+        gather_plain(0, H, V)
+        for d in (1, 2):
             gather_plain(d, 0, H)
             gather_plain(d, H, V)
-        gather_plain(2, FUSED, V - FUSED)
-        gather_plain(2, V - FUSED, V)
 
         gather_gated(3, 0, V)
-        multiply(0, 0, H)
-        gather_gated(2, 0, FUSED)
+        gather_gated(0, 0, H)
         multiply(0, H, V)
-        add(0, 0, H)
-        multiply(1, 0, H)
-        add(0, H, V)
-        multiply(1, H, V)
-        add(1, 0, H)
-        multiply(2, FUSED, V - FUSED)
-        multiply(2, V - FUSED, V)
-        add(1, H, V)
+        for d in (1, 2):
+            for v0 in (0, H):
+                multiply(d, v0, v0 + H)
+                add(d - 1, v0, v0 + H)
         add(2, 0, H)
         nc.scalar.dma_start(out=out[:, 0:H], in_=sums[2][:, 0:H])
         add(2, H, V)

@@ -43,7 +43,9 @@ def tile_picked_agg_lin_none_sub_l_kernel(tc, xT, w_words, w_scales, gate, pos1,
         psum = ctx.enter_context(tc.psum_pool(name="psum", bufs=1))
 
         lists = [keep.tile([P, V // 16], U16, name=f"list{d}") for d in range(D)]
-        gates = [keep.tile([P, V], F32, name=f"gates{d}") for d in range(D)]
+        first_gates = keep.tile([P, D - 1, V], F32)
+        last_gates = keep.tile([P, V], F32)
+        gates = [first_gates[:, d, :] for d in range(D - 1)] + [last_gates]
         w_codes = keep.tile([P, PASSES, M], U32, align_bytes=64)
         w_scale_rows = keep.tile([P, M], U8, align_bytes=64)
         y = keep.tile([P, T], F32)
@@ -77,13 +79,11 @@ def tile_picked_agg_lin_none_sub_l_kernel(tc, xT, w_words, w_scales, gate, pos1,
             if n + 1 < LAST:
                 load_w(nc.sync, n + 1)
         load_w(nc.sync, LAST)
-        nc.sync.dma_start(lists[3][:], positions[3])
-        nc.sync.dma_start(lists[0][:], positions[0])
-        nc.sync.dma_start(out=gates[3][:], in_=gate[3])
-        nc.sync.dma_start(lists[1][:], positions[1])
-        nc.sync.dma_start(lists[2][:], positions[2])
-        for d in range(3):
-            nc.sync.dma_start(out=gates[d][:], in_=gate[d])
+        for d in range(D - 1):
+            nc.sync.dma_start(lists[d][:], positions[d])
+        nc.sync.dma_start(out=first_gates[:], in_=gate[0 : D - 1].rearrange("d p v -> p d v"))
+        nc.sync.dma_start(lists[D - 1][:], positions[D - 1])
+        nc.sync.dma_start(out=last_gates[:], in_=gate[D - 1])
 
         grouped = [keep.tile([P, T, PACK], BF16, align_bytes=64, name=f"grouped{a}") for a in range(PASSES)]
         x_codes = [keep.tile([P, T], U32, align_bytes=64, name=f"x_codes{a}") for a in range(PASSES)]
@@ -119,9 +119,9 @@ def tile_picked_agg_lin_none_sub_l_kernel(tc, xT, w_words, w_scales, gate, pos1,
                 if a == LAST:
                     nc.scalar.copy(out=y[:, g0:g1], in_=banks[g][:, 0 : g1 - g0])
 
-        plain = [keep.tile([P, V], F32, name=f"plain{d}") for d in range(D - 1)]
+        plain = {d: keep.tile([P, V], F32, name=f"plain{d}") for d in range(1, D)}
         gated = [keep.tile([P, V], F32, name=f"gated{d}") for d in range(D)]
-        sums = [keep.tile([P, V], F32, name=f"sum{d}") for d in range(D - 1)]
+        sums = gated[0:1] + [keep.tile([P, V], F32, name=f"sum{d}") for d in range(1, D)]
 
         def neighbours(d, v0, v1):
             return y[:].indirect(lists[d][:, v0 // 16 : v1 // 16])
@@ -136,22 +136,25 @@ def tile_picked_agg_lin_none_sub_l_kernel(tc, xT, w_words, w_scales, gate, pos1,
             nc.vector.tensor_tensor(gated[d][:, v0:v1], plain[d][:, v0:v1], gates[d][:, v0:v1], MULT)
 
         def add(d, v0, v1):
-            so_far = gated[3] if d == 0 else sums[d - 1]
-            nc.vector.tensor_tensor(sums[d][:, v0:v1], so_far[:, v0:v1], gated[d][:, v0:v1], ADD)
+            nc.vector.tensor_tensor(sums[d][:, v0:v1], sums[d - 1][:, v0:v1], gated[d][:, v0:v1], ADD)
 
-        gather_plain(0, H, V)
-        for d in (1, 2):
+        gather_plain(1, H, V)
+        for d in (2, 3):
             gather_plain(d, 0, H)
             gather_plain(d, H, V)
 
-        gather_gated(3, 0, V)
-        gather_gated(0, 0, H)
-        multiply(0, H, V)
-        for d in (1, 2):
-            for v0 in (0, H):
-                multiply(d, v0, v0 + H)
-                add(d - 1, v0, v0 + H)
+        gather_gated(0, 0, V)
+        gather_gated(1, 0, H)
+        multiply(1, H, V)
+        multiply(2, 0, H)
+        add(1, 0, H)
+        multiply(2, H, V)
+        add(1, H, V)
+        multiply(3, 0, H)
         add(2, 0, H)
-        nc.scalar.dma_start(out=out[:, 0:H], in_=sums[2][:, 0:H])
         add(2, H, V)
-        nc.sync.dma_start(out=out[:, H:V], in_=sums[2][:, H:V])
+        multiply(3, H, V)
+        add(3, 0, H)
+        nc.scalar.dma_start(out=out[:, 0:H], in_=sums[3][:, 0:H])
+        add(3, H, V)
+        nc.sync.dma_start(out=out[:, H:V], in_=sums[3][:, H:V])

@@ -79,9 +79,11 @@ def tile_picked_agg_lin_none_sub_l_kernel(tc, xT, w_words, w_scales, gate, pos1,
             if n + 1 < LAST:
                 load_w(nc.sync, n + 1)
         load_w(nc.sync, LAST)
-        for d in range(D - 1):
+        for d in (1, 0, 2):
             nc.sync.dma_start(lists[d][:], positions[d])
-        nc.sync.dma_start(out=first_gates[:], in_=gate[0 : D - 1].rearrange("d p v -> p d v"))
+        first_rows = gate[0 : D - 1].rearrange("d p v -> p d v")
+        for first, step in ((0, 2), (1, 4), (3, 4)):
+            nc.sync.dma_start(out=first_gates[first:P:step], in_=first_rows[first:P:step])
         nc.sync.dma_start(lists[D - 1][:], positions[D - 1])
         nc.sync.dma_start(out=last_gates[:], in_=gate[D - 1])
 

@@ -78,9 +78,9 @@ def tile_picked_agg_lin_none_sub_l_kernel(tc, xT, w_words, w_scales, gate, pos1,
                     )
             if n + 1 < LAST:
                 load_w(nc.sync, n + 1)
-        load_w(nc.sync, LAST)
-        for d in (1, 0, 2):
+        for d in range(D - 1):
             nc.sync.dma_start(lists[d][:], positions[d])
+        load_w(nc.sync, LAST)
         first_rows = gate[0 : D - 1].rearrange("d p v -> p d v")
         for first, step in ((0, 2), (1, 4), (3, 4)):
             nc.sync.dma_start(out=first_gates[first:P:step], in_=first_rows[first:P:step])

@@ -78,9 +78,10 @@ def tile_picked_agg_lin_none_sub_l_kernel(tc, xT, w_words, w_scales, gate, pos1,
                     )
             if n + 1 < LAST:
                 load_w(nc.sync, n + 1)
-        for d in range(D - 1):
-            nc.sync.dma_start(lists[d][:], positions[d])
+        nc.sync.dma_start(lists[0][:], positions[0])
         load_w(nc.sync, LAST)
+        for d in (1, 2):
+            nc.sync.dma_start(lists[d][:], positions[d])
         first_rows = gate[0 : D - 1].rearrange("d p v -> p d v")
         for first, step in ((0, 2), (1, 4), (3, 4)):
             nc.sync.dma_start(out=first_gates[first:P:step], in_=first_rows[first:P:step])

@@ -158,6 +158,6 @@ def tile_picked_agg_lin_none_sub_l_kernel(tc, xT, w_words, w_scales, gate, pos1,
         add(2, H, V)
         multiply(3, H, V)
         add(3, 0, H)
-        nc.scalar.dma_start(out=out[:, 0:H], in_=sums[3][:, 0:H])
+        nc.sync.dma_start(out=out[:, 0:H], in_=sums[3][:, 0:H])
         add(3, H, V)
-        nc.sync.dma_start(out=out[:, H:V], in_=sums[3][:, H:V])
+        nc.scalar.dma_start(out=out[:, H:V], in_=sums[3][:, H:V])

@@ -27,11 +27,11 @@ H = V // 2
 GROUPS = ((0, 256), (256, 384), (384, 512))
 
 ALL = (0, T)
-LOADS = tuple(
-    (a, (0, 4), ALL, ((0, 128), (128, 256)), (256, T), ((0, 128), (128, 256), (256, T)), (0, 1, 2)) for a in range(LAST)
+LOADS = ((0, (0, 4), ALL, ((0, 256),), (256, T), ((0, 256), (256, T)), (0, 1, 2)),) + tuple(
+    (a, (0, 4), ALL, ((0, 128), (128, 256)), (256, T), ((0, 128), (128, 256), (256, T)), (0, 1, 2)) for a in range(1, LAST)
 ) + (
     (LAST, (0, 4), (0, 256), ((0, 64), (64, 128)), (128, 256), ((0, 64), (64, 128), (128, 256)), (0,)),
-    (LAST, (0, 4), (256, 384), (), (256, 384), ((256, 384),), (1,)),
+    (LAST, (0, 4), (256, 384), ((256, 288),), (288, 384), ((256, 384),), (1,)),
     (LAST, (0, 4), (384, 512), ((384, 448),), (448, 512), ((384, 448), (448, 512)), (2,)),
 )
 

from contextlib import ExitStack

import concourse.mybir as mybir

K, T, D, V, M = 2048, 512, 4, 256, 128
FLOPS = 2 * K * M * T + 2 * D * M * V

F32 = mybir.dt.float32
BF16 = mybir.dt.bfloat16
I32 = mybir.dt.int32
U32 = mybir.dt.uint32
U16 = mybir.dt.uint16
U8 = mybir.dt.uint8
FP8X4 = mybir.dt.float8_e4m3fn_x4
MULT = mybir.AluOpType.mult
ADD = mybir.AluOpType.add
COPY = mybir.ActivationFunctionType.Copy

P = 128
PACK = 4
K_PASS = P * PACK
PASSES = K // K_PASS
LAST = PASSES - 1
RUN = 4
H = V // 2

GROUPS = ((0, 256), (256, 384), (384, 512))

ALL = (0, T)
LOADS = ((0, (0, 4), ALL, ((0, 256),), (256, T), ((0, 256), (256, T)), (0, 1, 2)),) + tuple(
    (a, (0, 4), ALL, ((0, 128), (128, 256)), (256, T), ((0, 128), (128, 256), (256, T)), (0, 1, 2)) for a in range(1, LAST)
) + (
    (LAST, (0, 4), (0, 256), ((0, 64), (64, 128)), (128, 256), ((0, 64), (64, 128), (128, 256)), (0,)),
    (LAST, (0, 4), (256, 384), ((256, 288),), (288, 384), ((256, 384),), (1,)),
    (LAST, (0, 4), (384, 512), ((384, 448),), (448, 512), ((384, 448), (448, 512)), (2,)),
)


def tile_picked_agg_lin_none_sub_l_kernel(tc, xT, w_words, w_scales, gate, pos1, pos2, pos3, pos4, out):
    nc = tc.nc
    with ExitStack() as ctx:
        keep = ctx.enter_context(tc.tile_pool(name="keep", bufs=1))
        psum = ctx.enter_context(tc.psum_pool(name="psum", bufs=1))

        lists = [keep.tile([P, V // 16], U16, name=f"list{d}") for d in range(D)]
        first_gates = keep.tile([P, D - 1, V], F32)
        last_gates = keep.tile([P, V], F32)
        gates = [first_gates[:, d, :] for d in range(D - 1)] + [last_gates]
        w_codes = keep.tile([P, PASSES, M], U32, align_bytes=64)
        w_scale_rows = keep.tile([P, M], U8, align_bytes=64)
        y = keep.tile([P, T], F32)
        banks = [psum.tile([P, 512], F32, name=f"bank{g}") for g in range(len(GROUPS))]
        w_rows = w_words.rearrange("a p m r -> p a (m r)").bitcast(I32)
        positions = (pos1, pos2, pos3, pos4)

        def load_x(n):
            a, (j0, j1), (lo, hi) = LOADS[n][0:3]
            rows = xT[a * K_PASS : (a + 1) * K_PASS, :].rearrange("(p j) t -> p j t", j=PACK)
            raw = keep.tile([P, j1 - j0, hi - lo], F32, name=f"raw{n}")
            nc.sync.dma_start(out=raw[:], in_=rows[:, j0:j1, lo:hi])
            return raw

        def load_w(queue, a):
            queue.dma_start(out=w_codes[:, a, :].bitcast(I32), in_=w_rows[:, a, :])

        nc.gpsimd.memset(w_scale_rows[:].bitcast(I32), 0)

        load_w(nc.scalar, 0)

        raws = []
        for n in range(len(LOADS)):
            raws.append(load_x(n))
            if n == 0:
                for q in range(4):
                    nc.sync.dma_start(
                        out=w_scale_rows[32 * q : 32 * q + 16, :].bitcast(I32),
                        in_=w_scales[:, 4 * q : 4 * q + 4, :].bitcast(I32),
                    )
            if n + 1 < LAST:
                load_w(nc.sync, n + 1)
        nc.sync.dma_start(lists[0][:], positions[0])
        load_w(nc.sync, LAST)
        for d in (1, 2):
            nc.sync.dma_start(lists[d][:], positions[d])
        first_rows = gate[0 : D - 1].rearrange("d p v -> p d v")
        for first, step in ((0, 2), (1, 4), (3, 4)):
            nc.sync.dma_start(out=first_gates[first:P:step], in_=first_rows[first:P:step])
        nc.sync.dma_start(lists[D - 1][:], positions[D - 1])
        nc.sync.dma_start(out=last_gates[:], in_=gate[D - 1])

        grouped = [keep.tile([P, T, PACK], BF16, align_bytes=64, name=f"grouped{a}") for a in range(PASSES)]
        x_codes = [keep.tile([P, T], U32, align_bytes=64, name=f"x_codes{a}") for a in range(PASSES)]
        x_scales = [keep.tile([P, T], U8, align_bytes=64, name=f"x_scales{a}") for a in range(PASSES)]

        def interleave(copy, raw, a, j0, j1, lo, c0, c1):
            copy(
                out=grouped[a][:, c0:c1, j0:j1].rearrange("p (c i) j -> p c j i", i=RUN),
                in_=raw[:, :, c0 - lo : c1 - lo].rearrange("p j (c i) -> p c j i", i=RUN),
            )

        for raw, (a, (j0, j1), (lo, hi), on_vector, on_scalar, quantised, groups) in zip(raws, LOADS):
            interleave(nc.scalar.copy, raw, a, j0, j1, lo, *on_scalar)
            for c0, c1 in on_vector:
                interleave(nc.vector.tensor_copy, raw, a, j0, j1, lo, c0, c1)
            for c0, c1 in quantised:
                nc.vector.quantize_mx(
                    out=x_codes[a][:, c0:c1].bitcast(FP8X4),
                    scales=x_scales[a][:, c0:c1],
                    in_=grouped[a][:, c0:c1, :].rearrange("p c j -> p (c j)"),
                )
            for g in groups:
                g0, g1 = GROUPS[g]
                nc.tensor.matmul_mx(
                    out=banks[g][:, 0 : g1 - g0],
                    lhsT=w_codes[:, a, :].bitcast(FP8X4),
                    lhsT_scale=w_scale_rows[4 * a :, :],
                    rhs=x_codes[a][:, g0:g1].bitcast(FP8X4),
                    rhs_scale=x_scales[a][:, g0:g1],
                    start=(a == 0),
                    stop=(a == LAST),
                )
                if a == LAST:
                    nc.scalar.copy(out=y[:, g0:g1], in_=banks[g][:, 0 : g1 - g0])

        plain = {d: keep.tile([P, V], F32, name=f"plain{d}") for d in range(1, D)}
        gated = [keep.tile([P, V], F32, name=f"gated{d}") for d in range(D)]
        sums = gated[0:1] + [keep.tile([P, V], F32, name=f"sum{d}") for d in range(1, D)]

        def neighbours(d, v0, v1):
            return y[:].indirect(lists[d][:, v0 // 16 : v1 // 16])

        def gather_plain(d, v0, v1):
            nc.scalar.activation(plain[d][:, v0:v1], neighbours(d, v0, v1), COPY)

        def gather_gated(d, v0, v1):
            nc.vector.tensor_tensor(gated[d][:, v0:v1], neighbours(d, v0, v1), gates[d][:, v0:v1], MULT)

        def multiply(d, v0, v1):
            nc.vector.tensor_tensor(gated[d][:, v0:v1], plain[d][:, v0:v1], gates[d][:, v0:v1], MULT)

        def add(d, v0, v1):
            nc.vector.tensor_tensor(sums[d][:, v0:v1], sums[d - 1][:, v0:v1], gated[d][:, v0:v1], ADD)

        gather_plain(1, H, V)
        for d in (2, 3):
            gather_plain(d, 0, H)
            gather_plain(d, H, V)

        gather_gated(0, 0, V)
        gather_gated(1, 0, H)
        multiply(1, H, V)
        multiply(2, 0, H)
        add(1, 0, H)
        multiply(2, H, V)
        add(1, H, V)
        multiply(3, 0, H)
        add(2, 0, H)
        add(2, H, V)
        multiply(3, H, V)
        add(3, 0, H)
        nc.sync.dma_start(out=out[:, 0:H], in_=sums[3][:, 0:H])
        add(3, H, V)
        nc.scalar.dma_start(out=out[:, H:V], in_=sums[3][:, H:V])
